import numpy as np
import ml_dtypes


def mxq(x, axis, fmt="e4m3"):
    dtype, down = {"e4m3": (ml_dtypes.float8_e4m3fn, 7), "e5m2": (ml_dtypes.float8_e5m2, 14)}[fmt]
    v = np.moveaxis(np.asarray(x, np.float32).astype(ml_dtypes.bfloat16).astype(np.float64), axis, -1)
    blocks = v.reshape(v.shape[:-1] + (-1, 32))
    amax = np.abs(blocks).max(-1, keepdims=True)
    byte = np.maximum(np.where(amax > 0, np.frexp(amax)[1] - 1 + 127, 0) - down, 1)
    scale = np.exp2(byte - 127.0)
    codes = (blocks / scale).astype(np.float32).astype(dtype).astype(np.float64)
    return np.moveaxis((codes * scale).reshape(v.shape), -1, axis)


WIDE = False


def mx_kscale(k):
    if not WIDE:
        return np.ones(k)
    levels = np.array([10, -10, 5, -5, 0])
    if k % 512:
        return np.exp2(np.random.permutation(np.resize(levels, k // 32))).repeat(32)
    a = np.empty((k // 512, 16))
    for p in range(k // 512):
        a[p, :8] = np.random.permutation(np.resize(levels, 8))
        for g in range(8):
            far = levels[np.abs(levels - a[p, g]) >= 10]
            a[p, g + 8] = far[np.random.randint(len(far))]
    return np.exp2(a.ravel()).repeat(32)


BF16 = ml_dtypes.bfloat16


def bf(x):
    return np.asarray(x, np.float32).astype(BF16)


def f64(x):
    return np.asarray(x).astype(np.float64)


E2M1 = np.array([0.0, 0.5, 1.0, 1.5, 2.0, 3.0, 4.0, 6.0, -0.0, -0.5, -1.0, -1.5, -2.0, -3.0, -4.0, -6.0])


def pack_weight(w, fmt):
    k, n = w.shape
    w = f64(bf(w)).reshape(k // 32, 32, n)
    amax = np.abs(w).max(1)
    if fmt == "e4m3":
        byte = np.frexp(amax)[1] - 1 + 127 - 7
    else:
        mant, ex = np.frexp(amax / 6.0)
        byte = np.where(mant > 0.5, ex, ex - 1) + 127
    byte = np.clip(np.where(amax > 0, byte, 1), 1, 254)
    scaled = (w * np.exp2(127.0 - byte)[:, None, :]).reshape(k, n).astype(np.float32)
    by_word = np.ascontiguousarray(scaled.reshape(k // 512, 128, 4, n).transpose(0, 1, 3, 2))
    if fmt == "e4m3":
        words = by_word.astype(ml_dtypes.float8_e4m3fn).view(np.uint8)
    else:
        c = by_word.astype(ml_dtypes.float4_e2m1fn).view(np.uint8) & 0xF
        words = c[..., 0::2] | (c[..., 1::2] << 4)
    return np.ascontiguousarray(words), np.ascontiguousarray(byte.astype(np.uint8).reshape(k // 512, 16, n))


def unpack_weight(words, scales, fmt):
    g, p, n, _ = words.shape
    if fmt == "e4m3":
        vals = np.ascontiguousarray(words).view(ml_dtypes.float8_e4m3fn).astype(np.float64)
    else:
        nib = np.empty((g, p, n, 4), np.uint8)
        nib[..., 0::2] = words & 0xF
        nib[..., 1::2] = words >> 4
        vals = E2M1[nib]
    vals = vals * np.repeat(np.exp2(scales.astype(np.float64) - 127.0), 8, axis=1)[..., None]
    return vals.transpose(0, 1, 3, 2).reshape(g * 512, n)

E4M3FN = np.array([(-1.0 if i & 128 else 1.0) * ((1.0 + (i & 7) / 8.0) * 2.0 ** (((i >> 3) & 15) - 7) if i & 120 else (i & 7) * 2.0 ** -9) for i in range(256)])


def e4m3fn_bytes(y):
    return np.clip(np.asarray(y, np.float64), -448.0, 448.0).astype(np.float32).astype(ml_dtypes.float8_e4m3fn).view(np.uint8)


def e4m3fn_values(b):
    return E4M3FN[b]


N, D, J, V = 1024, 1024, 1024, 1536


def draw0():
    sh, se, t = mx_kscale(D), mx_kscale(D), mx_kscale(J)
    h = bf(np.random.standard_normal((N, D)) * sh)
    emb_words, emb_scales = pack_weight((np.random.standard_normal((V, D)) * se).T, "e4m3")
    u_words, u_scales = pack_weight(np.random.standard_normal((D, J)) / np.sqrt(D) / se[:, None], "e4m3")
    vp_words, vp_scales = pack_weight(np.random.standard_normal((D, J)) / np.sqrt(D) / sh[:, None], "e4m3")
    return {
        "h": h,
        "emb_words": emb_words,
        "emb_scales": emb_scales,
        "u_words": u_words,
        "u_scales": u_scales,
        "vp_words": vp_words,
        "vp_scales": vp_scales,
        "bj": bf(0.3 * np.random.standard_normal((2, J))),
        "gu": bf((1.0 + 0.1 * np.random.standard_normal(J)) / t),
        "gv": bf((1.0 + 0.1 * np.random.standard_normal(J)) * t),
    }


def joint_projection(x, w, b, g):
    y = x @ w
    return np.tanh(y + b[None, :]) * g[None, :]


def core(h, emb_words, emb_scales, u_words, u_scales, vp_words, vp_scales, bj, gu, gv):
    h, bj, gu, gv = f64(h), f64(bj), f64(gu), f64(gv)
    emb = unpack_weight(emb_words, emb_scales, "e4m3").T
    u = unpack_weight(u_words, u_scales, "e4m3")
    vp = unpack_weight(vp_words, vp_scales, "e4m3")
    joint_dim = u.shape[1]
    vocab = emb.shape[0]
    lab = joint_projection(emb, u, bj[0], gu)
    ctx = joint_projection(mxq(h, 1, "e4m3"), vp, bj[1], gv)
    scale = 2.0 / np.sqrt(joint_dim)
    s = scale * (mxq(ctx, 1, "e4m3") @ mxq(lab, 1, "e4m3").T)
    m = s.max(axis=1, keepdims=True)
    lse = m + np.log(np.exp(s - m).sum(axis=1, keepdims=True))
    return s - lse + np.log(vocab)


def setup_inputs():
    drawn = draw0()
    full = np.asarray(drawn['h']).astype(np.float64)
    scale = (np.abs(full).reshape(1024, 8, 128).max(axis=(2,)) / 448.0).astype(np.float32)
    given = {}
    for key, value in drawn.items():
        if key == 'h':
            given['h_bytes'] = e4m3fn_bytes(full / np.repeat(scale.astype(np.float64), 128, axis=1))
            given['h_scale'] = scale
        else:
            given[key] = value
    return given


def reference(h_bytes, h_scale, emb_words, emb_scales, u_words, u_scales, vp_words, vp_scales, bj, gu, gv):
    return core(e4m3fn_values(h_bytes) * np.repeat(h_scale.astype(np.float64), 128, axis=1), emb_words, emb_scales, u_words, u_scales, vp_words, vp_scales, bj, gu, gv)

@@ -1,0 +1,451 @@
+import math
+from contextlib import ExitStack
+
+import concourse.mybir as mybir
+from concourse.masks import make_identity
+
+N, D, J, V = 1024, 1024, 1024, 1536
+FLOPS = 2 * (V * D * J + N * D * J + N * J * V)
+
+F32 = mybir.dt.float32
+BF16 = mybir.dt.bfloat16
+I32 = mybir.dt.int32
+U32 = mybir.dt.uint32
+U8 = mybir.dt.uint8
+FP8 = mybir.dt.float8_e4m3fn
+X4 = mybir.dt.float8_e4m3fn_x4
+ACT = mybir.ActivationFunctionType
+ALU = mybir.AluOpType
+AX = mybir.AxisListType
+
+P = 128
+G = 2
+COLS = 512
+TILES = N // P
+KB = D // 128
+WIDEN_VECTOR = (6, 6, 6, 5, 4, 4, 4, 4)
+GATHER_VECTOR = (1, 3)
+SHARED_FROM = 6
+LN2 = math.log(2.0)
+SHIFT = math.log(V) + 3.0
+
+
+def tile_jointinputoutputembeddingtiedhead_d1p_kernel(
+    tc, h_bytes, h_scale, emb_words, emb_scales, u_words, u_scales, vp_words, vp_scales, bj, gu, gv, out
+):
+    nc = tc.nc
+    with ExitStack() as ctx:
+        keep = ctx.enter_context(tc.tile_pool(name="keep", bufs=1))
+        work = ctx.enter_context(tc.tile_pool(name="work", bufs=3))
+        stat = ctx.enter_context(tc.tile_pool(name="stat", bufs=6))
+        soft = ctx.enter_context(tc.tile_pool(name="soft", bufs=4))
+        banks = ctx.enter_context(tc.psum_pool(name="banks", bufs=8))
+
+        warm_out = keep.tile([P, 1], F32)
+
+        u_sc_raw = keep.tile([P, J], U8, align_bytes=64)
+        v_sc_raw = keep.tile([P, J], U8, align_bytes=64)
+        e_sc = keep.tile([P, V], U8, align_bytes=64)
+        nc.vector.memset(u_sc_raw[:].bitcast(I32), 0)
+        vec_raw = keep.tile([P, 512], BF16)
+        nc.vector.memset(vec_raw[:].bitcast(I32), 0)
+        nc.vector.memset(e_sc[:].bitcast(I32), 0)
+        nc.vector.memset(v_sc_raw[:].bitcast(I32), 0)
+        warm = keep.tile([P, 1], F32)
+        nc.vector.memset(warm[:], 0.0)
+        def load_scales(queue, tile_, src):
+            for q in range(4):
+                queue.dma_start(
+                    out=tile_[32 * q : 32 * q + 8, :].bitcast(I32),
+                    in_=src[:, 4 * q : 4 * q + 4, :].bitcast(I32),
+                )
+
+        load_scales(nc.scalar, u_sc_raw, u_scales)
+        ident = keep.tile([P, P], F32)
+        make_identity(nc, ident[:])
+        hs = keep.tile([P, TILES * KB], F32)
+        h_view = h_bytes.rearrange("(p i) k -> p (i k)", i=TILES)
+        nc.sync.dma_start(out=hs[:], in_=h_scale.rearrange("(p i) b -> p (i b)", i=TILES))
+        h_raw = []
+        for pair in range(4):
+            h_two = keep.tile([P, 2 * D], U8, align_bytes=64, name="h_raw%d" % pair)
+            h_raw.append(h_two)
+
+        def load_h(pair):
+            nc.sync.dma_start(out=h_raw[pair][:], in_=h_view[:, 2 * D * pair : 2 * D * (pair + 1)])
+
+        for pair in range(2):
+            load_h(pair)
+
+        def load_words(src, cols, tile_, g):
+            nc.sync.dma_start(
+                out=tile_[:, g, :],
+                in_=src[g].rearrange("p n t -> p (n t)").bitcast(I32)[:, cols],
+            )
+
+        nc.scalar.dma_start(out=vec_raw[0:4, :], in_=bj.rearrange("s j -> (s j)").rearrange("(x m) -> x m", x=4))
+        nc.scalar.dma_start(out=vec_raw[4:6, :], in_=gu.rearrange("(x m) -> x m", x=2))
+        nc.scalar.dma_start(out=vec_raw[6:8, :], in_=gv.rearrange("(x m) -> x m", x=2))
+        load_scales(nc.gpsimd, e_sc, emb_scales)
+        u_raw = keep.tile([P, G, J], I32, align_bytes=64)
+        v_raw = keep.tile([P, G, J], I32, align_bytes=64)
+        for g in range(G):
+            load_words(u_words, slice(0, J), u_raw, g)
+        e_words = []
+        for c in range(3):
+            e_chunk = keep.tile([P, G, COLS], I32, align_bytes=64, name="e_words%d" % c)
+            nc.sync.dma_start(
+                out=e_chunk[:],
+                in_=emb_words.rearrange("g p n t -> p g (n t)").bitcast(I32)[:, :, COLS * c : COLS * (c + 1)],
+            )
+            e_words.append(e_chunk)
+            if c == 0:
+                for pair in range(2, 4):
+                    load_h(pair)
+        for g in range(G):
+            load_words(vp_words, slice(0, J), v_raw, g)
+        load_scales(nc.gpsimd, v_sc_raw, vp_scales)
+        nc.scalar.activation(out=warm_out[:], in_=warm[:], func=ACT.Tanh)
+
+        vec_rows = keep.tile([P, 512], F32)
+        vecs = keep.tile([P, 8, 4], F32)
+        u_perm = keep.tile([P, G, J], I32, align_bytes=64)
+        v_perm = keep.tile([P, G, J], I32, align_bytes=64)
+        u_sc = keep.tile([P, J], U8, align_bytes=64)
+        v_sc = keep.tile([P, J], U8, align_bytes=64)
+
+        def permute_words(raw, dst, g):
+            nc.vector.tensor_copy(
+                out=dst[:, g, :].rearrange("p (b t q i) -> p b t q i", b=2, t=4, i=8),
+                in_=raw[:, g, :].rearrange("p (b q t i) -> p b t q i", b=2, t=4, i=8),
+            )
+
+        def permute_scales(sc_raw, sc_dst):
+            nc.vector.tensor_copy(
+                out=sc_dst[:].bitcast(I32).rearrange("p (b t q i) -> p b t q i", b=2, t=4, i=2),
+                in_=sc_raw[:].bitcast(I32).rearrange("p (b q t i) -> p b t q i", b=2, t=4, i=2),
+            )
+
+        h_grp = []
+        for half in range(2):
+            h_four = keep.tile([P, G, COLS, 2], F32, align_bytes=64, name="h_grp%d" % half)
+            h_grp.append(h_four)
+        h_codes = keep.tile([P, G, N], U32, align_bytes=64)
+        h_scales = keep.tile([P, G, N], U8, align_bytes=64)
+
+        def widen(i):
+            rows = work.tile([P, D], BF16, name="rows")
+            for j in range(KB):
+                at = D * (i % 2) + 128 * j
+                src = h_raw[i // 2][:, at : at + 128].bitcast(FP8)
+                dst = rows[:, 128 * j : 128 * (j + 1)]
+                col = hs[:, KB * i + j : KB * i + j + 1]
+                if j < WIDEN_VECTOR[i]:
+                    nc.vector.tensor_scalar(out=dst, in0=src, scalar1=col, scalar2=None, op0=ALU.mult)
+                else:
+                    nc.scalar.activation(out=dst, in_=src, func=ACT.Copy, scale=col)
+            return rows
+
+        def turn(rows):
+            words = rows[:].bitcast(F32)
+            bank = banks.tile([P, COLS], F32, name="bank")
+            for g in range(G):
+                for e in range(2):
+                    s0 = 128 * (2 * g + e)
+                    nc.tensor.transpose(bank[:, s0 : s0 + 128], words[:, 256 * g + e : 256 * (g + 1) : 2], ident[:])
+            return bank
+
+        def gather(i, bank, vector):
+            dst = h_grp[i // 4][:, :, 128 * (i % 4) : 128 * (i % 4 + 1), :]
+            src = bank[:].rearrange("p (g e r) -> p g r e", g=2, e=2)
+            if vector:
+                nc.vector.tensor_copy(out=dst, in_=src)
+            else:
+                nc.scalar.copy(out=dst, in_=src)
+
+        def quantize_h(half, g):
+            cols = slice(COLS * half, COLS * (half + 1))
+            nc.vector.quantize_mx(
+                out=h_codes[:, g, cols].bitcast(X4),
+                scales=h_scales[:, g, cols],
+                in_=h_grp[half][:, g].rearrange("p r e -> p (r e)").bitcast(BF16),
+            )
+
+        lab_codes = keep.tile([P, G, V], U32, align_bytes=64)
+        lab_scales = keep.tile([P, G, V], U8, align_bytes=64)
+        ctx_codes = keep.tile([P, G, N], U32, align_bytes=64)
+        ctx_scales = keep.tile([P, G, N], U8, align_bytes=64)
+
+        def project(side, jg, cc):
+            planes = work.tile([P, 4, COLS], F32, name="planes", bufs=3)
+            w, wsc = (u_perm, u_sc) if side == 0 else (v_perm, v_sc)
+            for t in range(4):
+                bank = banks.tile([P, COLS], F32, name="bank")
+                wcols = slice(512 * jg + 128 * t, 512 * jg + 128 * (t + 1))
+                for g in range(G):
+                    if side == 0:
+                        rhs = e_words[cc][:, g, :].bitcast(X4)
+                        rhs_scale = e_sc[4 * g :, COLS * cc : COLS * (cc + 1)]
+                    else:
+                        rhs = h_codes[:, g, COLS * cc : COLS * (cc + 1)].bitcast(X4)
+                        rhs_scale = h_scales[:, g, COLS * cc : COLS * (cc + 1)]
+                    nc.tensor.matmul_mx(
+                        out=bank[:],
+                        lhsT=w[:, g, wcols].bitcast(X4),
+                        lhsT_scale=wsc[4 * g :, wcols],
+                        rhs=rhs,
+                        rhs_scale=rhs_scale,
+                        start=(g == 0),
+                        stop=(g == G - 1),
+                    )
+                nc.scalar.activation(
+                    out=planes[:, t, :], in_=bank[:], func=ACT.Tanh, bias=vecs[:, 2 * side + jg, t : t + 1]
+                )
+            return planes
+
+        def apply_gain(side, jg, planes, engine):
+            four = work.tile([P, COLS, 4], BF16, align_bytes=64, name="four", bufs=3)
+            engine.tensor_tensor(
+                out=four[:].rearrange("p (c i) t -> p c t i", i=4),
+                in0=planes[:].rearrange("p t (c i) -> p c t i", i=4),
+                in1=vecs[:, 4 + 2 * side + jg, :].unsqueeze(1).unsqueeze(3).to_broadcast([P, COLS // 4, 4, 4]),
+                op=ALU.mult,
+            )
+            return four
+
+        def quantize_joint(side, jg, cc, four):
+            codes, scales = (lab_codes, lab_scales) if side == 0 else (ctx_codes, ctx_scales)
+            cols = slice(COLS * cc, COLS * (cc + 1))
+            nc.vector.quantize_mx(
+                out=codes[:, jg, cols].bitcast(X4),
+                scales=scales[:, jg, cols],
+                in_=four[:].rearrange("p c t -> p (c t)"),
+            )
+
+        out_view = out.rearrange("(p i) v -> i p v", i=TILES)
+
+        def scores(i, c):
+            bank = banks.tile([P, COLS], F32, name="bank")
+            for g in range(G):
+                nc.tensor.matmul_mx(
+                    out=bank[:],
+                    lhsT=ctx_codes[:, g, P * i : P * (i + 1)].bitcast(X4),
+                    lhsT_scale=ctx_scales[:, g, P * i : P * (i + 1)],
+                    rhs=lab_codes[:, g, COLS * c : COLS * (c + 1)].bitcast(X4),
+                    rhs_scale=lab_scales[:, g, COLS * c : COLS * (c + 1)],
+                    start=(g == 0),
+                    stop=(g == G - 1),
+                )
+            return bank
+
+        rows_of = {}
+
+        def start_tile(i):
+            r = {}
+            r["s"] = soft.tile([P, V], F32, name="s", bufs=6)
+            r["tops"] = stat.tile([P, 8], F32, name="tops")
+            r["sums"] = stat.tile([P, 8], F32, name="sums")
+            r["y"] = []
+            for k in range(4):
+                yk = stat.tile([P, 1], F32, name="y%d" % k)
+                r["y"].append(yk)
+            r["e"] = []
+            for k in range(3):
+                ek = stat.tile([P, 1], F32, name="e%d" % k)
+                r["e"].append(ek)
+            r["neg_top"] = stat.tile([P, 1], F32, name="neg_top")
+            r["total"] = stat.tile([P, 1], F32, name="total")
+            r["add"] = stat.tile([P, 1], F32, name="add")
+            rows_of[i] = r
+
+        def take(i, c, bank):
+            r = rows_of[i]
+            nc.vector.tensor_scalar(
+                out=r["s"][:, COLS * c : COLS * (c + 1)],
+                in0=bank[:],
+                scalar1=2.0 / math.sqrt(J),
+                scalar2=None,
+                op0=ALU.mult,
+                op1=ALU.max,
+                accum_out=r["tops"][:, c : c + 1],
+            )
+
+        def top(i):
+            r = rows_of[i]
+            nc.vector.tensor_reduce(out=r["neg_top"][:], in_=r["tops"][:, 0:3], axis=AX.X, op=ALU.max, negate=True)
+
+        def exp_piece(i, c):
+            r = rows_of[i]
+            junk = work.tile([P, COLS], BF16, name="junk")
+            nc.scalar.activation(
+                out=junk[:],
+                in_=r["s"][:, COLS * c : COLS * (c + 1)],
+                func=ACT.Exp,
+                bias=r["neg_top"][:],
+                accum_out=r["sums"][:, c : c + 1],
+            )
+
+        def total(i):
+            r = rows_of[i]
+            nc.vector.tensor_reduce(out=r["total"][:], in_=r["sums"][:, 0:3], axis=AX.X, op=ALU.add)
+
+        def guess(i):
+            r = rows_of[i]
+            nc.vector.tensor_scalar(
+                out=r["y"][0][:],
+                in0=r["total"][:].bitcast(I32),
+                scalar1=LN2 / 2.0**23,
+                scalar2=-(127.0 - 0.043) * LN2 - SHIFT,
+                op0=ALU.mult,
+                op1=ALU.add,
+            )
+
+        def newton_exp(i, k):
+            r = rows_of[i]
+            nc.scalar.activation(out=r["e"][k][:], in_=r["y"][k][:], func=ACT.Exp, scale=-1.0, bias=k - SHIFT)
+
+        def newton_add(i, k):
+            r = rows_of[i]
+            nc.vector.scalar_tensor_tensor(
+                out=r["y"][k + 1][:], in0=r["e"][k][:], scalar=r["total"][:], in1=r["y"][k][:], op0=ALU.mult, op1=ALU.add
+            )
+
+        def vectors():
+            nc.scalar.copy(
+                out=vec_rows[:].rearrange("p (t q i) -> p t q i", t=4, i=8),
+                in_=vec_raw[:].rearrange("p (q t i) -> p t q i", t=4, i=8),
+            )
+            bank = banks.tile([P, COLS], F32, name="bank")
+            for t in range(4):
+                nc.tensor.transpose(bank[:, 128 * t : 128 * (t + 1)], vec_rows[:, 128 * t : 128 * (t + 1)], ident[:])
+            nc.scalar.copy(
+                out=vecs[:], in_=bank[:].rearrange("p (t r) -> p r t", t=4)[:, 0:8, :]
+            )
+
+        def gain_scalar(side, jg, planes):
+            rounded = work.tile([P, 4, COLS], BF16, name="rounded", bufs=2)
+            for t in range(4):
+                nc.scalar.activation(
+                    out=rounded[:, t, :], in_=planes[:, t, :], func=ACT.Copy, scale=vecs[:, 4 + 2 * side + jg, t : t + 1]
+                )
+            four = work.tile([P, COLS, 4], BF16, align_bytes=64, name="four", bufs=3)
+            nc.vector.tensor_copy(
+                out=four[:].rearrange("p (c i) t -> p c t i", i=4),
+                in_=rounded[:].rearrange("p t (c i) -> p c t i", i=4),
+            )
+            return four
+
+        def finish(i):
+            r = rows_of[i]
+            nc.scalar.activation(
+                out=r["add"][:], in_=r["y"][3][:], func=ACT.Identity, scale=-1.0, bias=r["neg_top"][:]
+            )
+            res = soft.tile([P, V], F32, name="res", bufs=3)
+            if i < SHARED_FROM:
+                nc.gpsimd.tensor_scalar(
+                    out=res[:], in0=r["s"][:], scalar1=1.0, scalar2=r["add"][:], op0=ALU.mult, op1=ALU.add
+                )
+                nc.sync.dma_start(out=out_view[i], in_=res[:])
+            else:
+                a, b = 832, 1232
+                nc.vector.tensor_scalar(
+                    out=res[:, 0:a], in0=r["s"][:, 0:a], scalar1=r["add"][:], scalar2=None, op0=ALU.add
+                )
+                nc.sync.dma_start(out=out_view[i][:, 0:a], in_=res[:, 0:a])
+                nc.scalar.activation(
+                    out=res[:, a:b], in_=r["s"][:, a:b], func=ACT.Identity, bias=r["add"][:]
+                )
+                nc.sync.dma_start(out=out_view[i][:, a:b], in_=res[:, a:b])
+                nc.gpsimd.tensor_scalar(
+                    out=res[:, b:V], in0=r["s"][:, b:V], scalar1=1.0, scalar2=r["add"][:], op0=ALU.mult, op1=ALU.add
+                )
+                nc.sync.dma_start(out=out_view[i][:, b:V], in_=res[:, b:V])
+
+        with tc.manual_schedule():
+            turned = {}
+            for i in range(4 + 1):
+                if i < 4:
+                    turned[i] = turn(widen(i))
+                if i == 1:
+                    vectors()
+                if i == 3:
+                    permute_scales(u_sc_raw, u_sc)
+                    permute_words(u_raw, u_perm, 0)
+                if i == 4:
+                    permute_words(u_raw, u_perm, 1)
+                if i >= 1:
+                    gather(i - 1, turned[i - 1], i - 1 in GATHER_VECTOR)
+            groups = [(0, jg, cc) for cc in range(3) for jg in range(G)]
+            groups += [(1, jg, cc) for cc in range(2) for jg in range(G)]
+            planes_of = {}
+            four_of = {}
+            rows_left = {}
+            for n in range(len(groups) + 2):
+                if n < len(groups):
+                    planes_of[n] = project(*groups[n])
+                i = 4 + n - 0
+                if 4 <= i < TILES:
+                    rows_left[i] = widen(i)
+                if 4 <= i - 1 < TILES:
+                    turned[i - 1] = turn(rows_left[i - 1])
+                if 4 <= i - 2 < TILES:
+                    gather(i - 2, turned[i - 2], i - 2 in GATHER_VECTOR)
+                if n == 0:
+                    quantize_h(0, 0)
+                    quantize_h(0, 1)
+                if n == 7:
+                    quantize_h(1, 0)
+                    quantize_h(1, 1)
+                if n == 3:
+                    permute_scales(v_sc_raw, v_sc)
+                    for g in range(G):
+                        permute_words(v_raw, v_perm, g)
+                if 1 <= n <= len(groups):
+                    m = n - 1
+                    if m in []:
+                        four_of[m] = gain_scalar(groups[m][0], groups[m][1], planes_of[m])
+                    else:
+                        four_of[m] = apply_gain(
+                            groups[m][0], groups[m][1], planes_of[m], nc.gpsimd if m in [9] else nc.vector
+                        )
+                if n >= 2 and n - 2 not in [9]:
+                    quantize_joint(*groups[n - 2], four_of[n - 2])
+            for r in range(TILES + 4):
+                new, old1, old2, old3, old4 = (x if 0 <= x < TILES else None for x in range(r, r - 5, -1))
+                if new is not None:
+                    start_tile(new)
+                if r in [3]:
+                    m = [9][[3].index(r)]
+                    quantize_joint(*groups[m], four_of[m])
+                if old4 is not None:
+                    finish(old4)
+                if old3 is not None:
+                    newton_exp(old3, 1)
+                if old2 is not None:
+                    total(old2)
+                if new is not None:
+                    take(new, 0, scores(new, 0))
+                if old1 is not None:
+                    exp_piece(old1, 0)
+                if old2 is not None:
+                    guess(old2)
+                if old3 is not None:
+                    newton_add(old3, 1)
+                if new is not None:
+                    take(new, 1, scores(new, 1))
+                if old1 is not None:
+                    exp_piece(old1, 1)
+                if old2 is not None:
+                    newton_exp(old2, 0)
+                if old3 is not None:
+                    newton_exp(old3, 2)
+                if new is not None:
+                    take(new, 2, scores(new, 2))
+                if old1 is not None:
+                    exp_piece(old1, 2)
+                if old2 is not None:
+                    newton_add(old2, 0)
+                if old3 is not None:
+                    newton_add(old3, 2)
+                if new is not None:
+                    top(new)

@@ -23,9 +23,12 @@ G = 2
 COLS = 512
 TILES = N // P
 KB = D // 128
-WIDEN_VECTOR = (6, 6, 6, 5, 4, 4, 4, 4)
+WIDEN_VECTOR = (6, 6, 5, 5, 4, 4, 4, 4)
 GATHER_VECTOR = (1, 3)
 SHARED_FROM = 6
+GAIN_ENGINE = "VVVVVVVVAP"
+LATE = {1: 8, 3: 9}
+WIDEN_AT = {2: 0, 3: 0, 4: 1, 5: 2, 6: 3, 7: 4}
 LN2 = math.log(2.0)
 SHIFT = math.log(V) + 3.0
 
@@ -60,7 +63,6 @@ def tile_jointinputoutputembeddingtiedhead_d1p_kernel(
                     in_=src[:, 4 * q : 4 * q + 4, :].bitcast(I32),
                 )
 
-        load_scales(nc.scalar, u_sc_raw, u_scales)
         ident = keep.tile([P, P], F32)
         make_identity(nc, ident[:])
         hs = keep.tile([P, TILES * KB], F32)
@@ -74,50 +76,44 @@ def tile_jointinputoutputembeddingtiedhead_d1p_kernel(
         def load_h(pair):
             nc.sync.dma_start(out=h_raw[pair][:], in_=h_view[:, 2 * D * pair : 2 * D * (pair + 1)])
 
-        for pair in range(2):
-            load_h(pair)
+        u_raw = [keep.tile([P, G, COLS], I32, align_bytes=64, name="u_raw%d" % b) for b in range(2)]
+        v_raw = [keep.tile([P, G, COLS], I32, align_bytes=64, name="v_raw%d" % b) for b in range(2)]
+        e_words = [keep.tile([P, G, COLS], I32, align_bytes=64, name="e_words%d" % c) for c in range(3)]
 
-        def load_words(src, cols, tile_, g):
-            nc.sync.dma_start(
-                out=tile_[:, g, :],
-                in_=src[g].rearrange("p n t -> p (n t)").bitcast(I32)[:, cols],
-            )
+        def load_words(src, block, tile_):
+            words = src.rearrange("g p n t -> p g (n t)").bitcast(I32)
+            nc.sync.dma_start(out=tile_[:], in_=words[:, :, COLS * block : COLS * (block + 1)])
 
+        load_scales(nc.gpsimd, e_sc, emb_scales)
+        load_h(0)
+        load_words(u_words, 0, u_raw[0])
+        load_words(emb_words, 0, e_words[0])
+        load_scales(nc.scalar, u_sc_raw, u_scales)
         nc.scalar.dma_start(out=vec_raw[0:4, :], in_=bj.rearrange("s j -> (s j)").rearrange("(x m) -> x m", x=4))
         nc.scalar.dma_start(out=vec_raw[4:6, :], in_=gu.rearrange("(x m) -> x m", x=2))
         nc.scalar.dma_start(out=vec_raw[6:8, :], in_=gv.rearrange("(x m) -> x m", x=2))
-        load_scales(nc.gpsimd, e_sc, emb_scales)
-        u_raw = keep.tile([P, G, J], I32, align_bytes=64)
-        v_raw = keep.tile([P, G, J], I32, align_bytes=64)
-        for g in range(G):
-            load_words(u_words, slice(0, J), u_raw, g)
-        e_words = []
-        for c in range(3):
-            e_chunk = keep.tile([P, G, COLS], I32, align_bytes=64, name="e_words%d" % c)
-            nc.sync.dma_start(
-                out=e_chunk[:],
-                in_=emb_words.rearrange("g p n t -> p g (n t)").bitcast(I32)[:, :, COLS * c : COLS * (c + 1)],
-            )
-            e_words.append(e_chunk)
-            if c == 0:
-                for pair in range(2, 4):
-                    load_h(pair)
-        for g in range(G):
-            load_words(vp_words, slice(0, J), v_raw, g)
+        load_h(1)
+        load_words(u_words, 1, u_raw[1])
+        load_h(2)
+        load_h(3)
+        load_words(emb_words, 1, e_words[1])
+        load_words(emb_words, 2, e_words[2])
+        load_words(vp_words, 0, v_raw[0])
+        load_words(vp_words, 1, v_raw[1])
         load_scales(nc.gpsimd, v_sc_raw, vp_scales)
         nc.scalar.activation(out=warm_out[:], in_=warm[:], func=ACT.Tanh)
 
         vec_rows = keep.tile([P, 512], F32)
         vecs = keep.tile([P, 8, 4], F32)
-        u_perm = keep.tile([P, G, J], I32, align_bytes=64)
-        v_perm = keep.tile([P, G, J], I32, align_bytes=64)
+        u_perm = [keep.tile([P, G, COLS], I32, align_bytes=64, name="u_perm%d" % b) for b in range(2)]
+        v_perm = [keep.tile([P, G, COLS], I32, align_bytes=64, name="v_perm%d" % b) for b in range(2)]
         u_sc = keep.tile([P, J], U8, align_bytes=64)
         v_sc = keep.tile([P, J], U8, align_bytes=64)
 
-        def permute_words(raw, dst, g):
+        def permute_words(raw, dst, b):
             nc.vector.tensor_copy(
-                out=dst[:, g, :].rearrange("p (b t q i) -> p b t q i", b=2, t=4, i=8),
-                in_=raw[:, g, :].rearrange("p (b q t i) -> p b t q i", b=2, t=4, i=8),
+                out=dst[b][:].rearrange("p g (t q i) -> p g t q i", t=4, i=8),
+                in_=raw[b][:].rearrange("p g (q t i) -> p g t q i", t=4, i=8),
             )
 
         def permute_scales(sc_raw, sc_dst):
@@ -191,7 +187,7 @@ def tile_jointinputoutputembeddingtiedhead_d1p_kernel(
                         rhs_scale = h_scales[:, g, COLS * cc : COLS * (cc + 1)]
                     nc.tensor.matmul_mx(
                         out=bank[:],
-                        lhsT=w[:, g, wcols].bitcast(X4),
+                        lhsT=w[jg][:, g, 128 * t : 128 * (t + 1)].bitcast(X4),
                         lhsT_scale=wsc[4 * g :, wcols],
                         rhs=rhs,
                         rhs_scale=rhs_scale,
@@ -203,13 +199,23 @@ def tile_jointinputoutputembeddingtiedhead_d1p_kernel(
                 )
             return planes
 
-        def apply_gain(side, jg, planes, engine):
+        def apply_gain(n, side, jg, planes):
+            rounded = work.tile([P, 4, COLS], BF16, align_bytes=64, name="rounded")
+            for t in range(4):
+                dst, src, gain = rounded[:, t, :], planes[:, t, :], vecs[:, 4 + 2 * side + jg, t : t + 1]
+                if GAIN_ENGINE[n] == "V":
+                    nc.vector.tensor_scalar(out=dst, in0=src, scalar1=gain, scalar2=None, op0=ALU.mult)
+                elif GAIN_ENGINE[n] == "A":
+                    nc.scalar.activation(out=dst, in_=src, func=ACT.Copy, scale=gain)
+                else:
+                    nc.gpsimd.tensor_scalar(out=dst, in0=src, scalar1=gain, scalar2=0.0, op0=ALU.mult, op1=ALU.add)
+            return rounded
+
+        def interleave(rounded):
             four = work.tile([P, COLS, 4], BF16, align_bytes=64, name="four", bufs=3)
-            engine.tensor_tensor(
-                out=four[:].rearrange("p (c i) t -> p c t i", i=4),
-                in0=planes[:].rearrange("p t (c i) -> p c t i", i=4),
-                in1=vecs[:, 4 + 2 * side + jg, :].unsqueeze(1).unsqueeze(3).to_broadcast([P, COLS // 4, 4, 4]),
-                op=ALU.mult,
+            nc.vector.tensor_copy(
+                out=four[:],
+                in_=rounded[:].rearrange("p t c -> p c t"),
             )
             return four
 
@@ -322,25 +328,12 @@ def tile_jointinputoutputembeddingtiedhead_d1p_kernel(
                 out=vecs[:], in_=bank[:].rearrange("p (t r) -> p r t", t=4)[:, 0:8, :]
             )
 
-        def gain_scalar(side, jg, planes):
-            rounded = work.tile([P, 4, COLS], BF16, name="rounded", bufs=2)
-            for t in range(4):
-                nc.scalar.activation(
-                    out=rounded[:, t, :], in_=planes[:, t, :], func=ACT.Copy, scale=vecs[:, 4 + 2 * side + jg, t : t + 1]
-                )
-            four = work.tile([P, COLS, 4], BF16, align_bytes=64, name="four", bufs=3)
-            nc.vector.tensor_copy(
-                out=four[:].rearrange("p (c i) t -> p c t i", i=4),
-                in_=rounded[:].rearrange("p t (c i) -> p c t i", i=4),
-            )
-            return four
-
         def finish(i):
             r = rows_of[i]
             nc.scalar.activation(
                 out=r["add"][:], in_=r["y"][3][:], func=ACT.Identity, scale=-1.0, bias=r["neg_top"][:]
             )
-            res = soft.tile([P, V], F32, name="res", bufs=3)
+            res = soft.tile([P, V], F32, name="res", bufs=5)
             if i < SHARED_FROM:
                 nc.gpsimd.tensor_scalar(
                     out=res[:], in0=r["s"][:], scalar1=1.0, scalar2=r["add"][:], op0=ALU.mult, op1=ALU.add
@@ -363,60 +356,56 @@ def tile_jointinputoutputembeddingtiedhead_d1p_kernel(
 
         with tc.manual_schedule():
             turned = {}
-            for i in range(4 + 1):
-                if i < 4:
+            for i in range(2 + 1):
+                if i < 2:
                     turned[i] = turn(widen(i))
                 if i == 1:
                     vectors()
-                if i == 3:
-                    permute_scales(u_sc_raw, u_sc)
-                    permute_words(u_raw, u_perm, 0)
-                if i == 4:
-                    permute_words(u_raw, u_perm, 1)
                 if i >= 1:
                     gather(i - 1, turned[i - 1], i - 1 in GATHER_VECTOR)
+            permute_scales(u_sc_raw, u_sc)
+            permute_words(u_raw, u_perm, 0)
             groups = [(0, jg, cc) for cc in range(3) for jg in range(G)]
             groups += [(1, jg, cc) for cc in range(2) for jg in range(G)]
             planes_of = {}
+            rounded_of = {}
             four_of = {}
             rows_left = {}
-            for n in range(len(groups) + 2):
+            for n in range(len(groups) + 1):
                 if n < len(groups):
                     planes_of[n] = project(*groups[n])
-                i = 4 + n - 0
-                if 4 <= i < TILES:
-                    rows_left[i] = widen(i)
-                if 4 <= i - 1 < TILES:
-                    turned[i - 1] = turn(rows_left[i - 1])
-                if 4 <= i - 2 < TILES:
-                    gather(i - 2, turned[i - 2], i - 2 in GATHER_VECTOR)
-                if n == 0:
+                for i in range(2, TILES):
+                    if WIDEN_AT[i] == n:
+                        rows_left[i] = widen(i)
+                    if WIDEN_AT[i] + 1 == n:
+                        turned[i] = turn(rows_left[i])
+                    if WIDEN_AT[i] + 2 == n:
+                        gather(i, turned[i], i in GATHER_VECTOR)
+                if n == 3:
                     quantize_h(0, 0)
                     quantize_h(0, 1)
                 if n == 7:
                     quantize_h(1, 0)
                     quantize_h(1, 1)
-                if n == 3:
+                if n == 4:
                     permute_scales(v_sc_raw, v_sc)
-                    for g in range(G):
-                        permute_words(v_raw, v_perm, g)
+                    permute_words(v_raw, v_perm, 0)
+                    permute_words(v_raw, v_perm, 1)
+                if n == 0:
+                    permute_words(u_raw, u_perm, 1)
                 if 1 <= n <= len(groups):
-                    m = n - 1
-                    if m in []:
-                        four_of[m] = gain_scalar(groups[m][0], groups[m][1], planes_of[m])
-                    else:
-                        four_of[m] = apply_gain(
-                            groups[m][0], groups[m][1], planes_of[m], nc.gpsimd if m in [9] else nc.vector
-                        )
-                if n >= 2 and n - 2 not in [9]:
-                    quantize_joint(*groups[n - 2], four_of[n - 2])
+                    rounded_of[n - 1] = apply_gain(n - 1, groups[n - 1][0], groups[n - 1][1], planes_of[n - 1])
+                if 3 <= n and n - 3 < 8:
+                    quantize_joint(*groups[n - 3], four_of[n - 3])
+                if 2 <= n and n - 2 < 8:
+                    four_of[n - 2] = interleave(rounded_of[n - 2])
             for r in range(TILES + 4):
                 new, old1, old2, old3, old4 = (x if 0 <= x < TILES else None for x in range(r, r - 5, -1))
                 if new is not None:
                     start_tile(new)
-                if r in [3]:
-                    m = [9][[3].index(r)]
-                    quantize_joint(*groups[m], four_of[m])
+                late = LATE.get(r)
+                if late is not None:
+                    quantize_joint(*groups[late], four_of[late])
                 if old4 is not None:
                     finish(old4)
                 if old3 is not None:
@@ -431,6 +420,9 @@ def tile_jointinputoutputembeddingtiedhead_d1p_kernel(
                     guess(old2)
                 if old3 is not None:
                     newton_add(old3, 1)
+                late = LATE.get(r + 1)
+                if late is not None:
+                    four_of[late] = interleave(rounded_of[late])
                 if new is not None:
                     take(new, 1, scores(new, 1))
                 if old1 is not None:

@@ -23,14 +23,14 @@ G = 2
 COLS = 512
 TILES = N // P
 KB = D // 128
-WIDEN_VECTOR = (6, 6, 5, 5, 4, 4, 4, 4)
-GATHER_VECTOR = (1, 3)
-SHARED_FROM = 6
-GAIN_ENGINE = "VVVVVVVVAP"
+WIDEN_VECTOR = (8, 8, 6, 6, 4, 4, 4, 4)
+GATHER_VECTOR = (98, 99)
+SHARED_FROM = 5
+GAIN_ENGINE = "VVVVVVVVAA"
 LATE = {1: 8, 3: 9}
-WIDEN_AT = {2: 0, 3: 0, 4: 1, 5: 2, 6: 3, 7: 4}
+WIDEN_AT = {4: 0, 5: 1, 6: 2, 7: 3}
 LN2 = math.log(2.0)
-SHIFT = math.log(V) + 3.0
+GUESS = (256.0 + 127.0 - 0.043) * LN2 + math.log(V) + 3.0
 
 
 def tile_jointinputoutputembeddingtiedhead_d1p_kernel(
@@ -56,8 +56,8 @@ def tile_jointinputoutputembeddingtiedhead_d1p_kernel(
         nc.vector.memset(v_sc_raw[:].bitcast(I32), 0)
         warm = keep.tile([P, 1], F32)
         nc.vector.memset(warm[:], 0.0)
-        def load_scales(queue, tile_, src):
-            for q in range(4):
+        def load_scales(queue, tile_, src, quadrants=range(4)):
+            for q in quadrants:
                 queue.dma_start(
                     out=tile_[32 * q : 32 * q + 8, :].bitcast(I32),
                     in_=src[:, 4 * q : 4 * q + 4, :].bitcast(I32),
@@ -84,15 +84,16 @@ def tile_jointinputoutputembeddingtiedhead_d1p_kernel(
             words = src.rearrange("g p n t -> p g (n t)").bitcast(I32)
             nc.sync.dma_start(out=tile_[:], in_=words[:, :, COLS * block : COLS * (block + 1)])
 
-        load_scales(nc.gpsimd, e_sc, emb_scales)
         load_h(0)
+        load_h(1)
         load_words(u_words, 0, u_raw[0])
-        load_words(emb_words, 0, e_words[0])
-        load_scales(nc.scalar, u_sc_raw, u_scales)
         nc.scalar.dma_start(out=vec_raw[0:4, :], in_=bj.rearrange("s j -> (s j)").rearrange("(x m) -> x m", x=4))
         nc.scalar.dma_start(out=vec_raw[4:6, :], in_=gu.rearrange("(x m) -> x m", x=2))
         nc.scalar.dma_start(out=vec_raw[6:8, :], in_=gv.rearrange("(x m) -> x m", x=2))
-        load_h(1)
+        load_scales(nc.scalar, u_sc_raw, u_scales)
+        load_scales(nc.scalar, e_sc, emb_scales, range(2, 4))
+        load_scales(nc.gpsimd, e_sc, emb_scales, range(2))
+        load_words(emb_words, 0, e_words[0])
         load_words(u_words, 1, u_raw[1])
         load_h(2)
         load_h(3)
@@ -199,24 +200,23 @@ def tile_jointinputoutputembeddingtiedhead_d1p_kernel(
                 )
             return planes
 
-        def apply_gain(n, side, jg, planes):
-            rounded = work.tile([P, 4, COLS], BF16, align_bytes=64, name="rounded")
+        def scalar_gain(side, jg, planes):
+            rounded = work.tile([P, 4, COLS], BF16, align_bytes=64, name="rounded", bufs=2)
             for t in range(4):
-                dst, src, gain = rounded[:, t, :], planes[:, t, :], vecs[:, 4 + 2 * side + jg, t : t + 1]
-                if GAIN_ENGINE[n] == "V":
-                    nc.vector.tensor_scalar(out=dst, in0=src, scalar1=gain, scalar2=None, op0=ALU.mult)
-                elif GAIN_ENGINE[n] == "A":
-                    nc.scalar.activation(out=dst, in_=src, func=ACT.Copy, scale=gain)
-                else:
-                    nc.gpsimd.tensor_scalar(out=dst, in0=src, scalar1=gain, scalar2=0.0, op0=ALU.mult, op1=ALU.add)
+                nc.scalar.activation(
+                    out=rounded[:, t, :], in_=planes[:, t, :], func=ACT.Copy, scale=vecs[:, 4 + 2 * side + jg, t : t + 1]
+                )
             return rounded
 
-        def interleave(rounded):
+        def interleave(n, side, jg, source):
             four = work.tile([P, COLS, 4], BF16, align_bytes=64, name="four", bufs=3)
-            nc.vector.tensor_copy(
-                out=four[:],
-                in_=rounded[:].rearrange("p t c -> p c t"),
-            )
+            dst = four[:].rearrange("p (c i) t -> p c t i", i=4)
+            src = source[:].rearrange("p t (c i) -> p c t i", i=4)
+            if GAIN_ENGINE[n] == "A":
+                nc.vector.tensor_copy(out=dst, in_=src)
+            else:
+                gain = vecs[:, 4 + 2 * side + jg, :].unsqueeze(1).unsqueeze(3).to_broadcast([P, COLS // 4, 4, 4])
+                nc.vector.tensor_tensor(out=dst, in0=src, in1=gain, op=ALU.mult)
             return four
 
         def quantize_joint(side, jg, cc, four):
@@ -251,16 +251,10 @@ def tile_jointinputoutputembeddingtiedhead_d1p_kernel(
             r["s"] = soft.tile([P, V], F32, name="s", bufs=6)
             r["tops"] = stat.tile([P, 8], F32, name="tops")
             r["sums"] = stat.tile([P, 8], F32, name="sums")
-            r["y"] = []
-            for k in range(4):
-                yk = stat.tile([P, 1], F32, name="y%d" % k)
-                r["y"].append(yk)
-            r["e"] = []
-            for k in range(3):
-                ek = stat.tile([P, 1], F32, name="e%d" % k)
-                r["e"].append(ek)
+            for key in ("v0", "v1", "v2", "e0", "e1", "e2", "near"):
+                r[key] = stat.tile([P, 1], F32, name=key)
             r["neg_top"] = stat.tile([P, 1], F32, name="neg_top")
-            r["total"] = stat.tile([P, 1], F32, name="total")
+            r["minus_sum"] = stat.tile([P, 1], F32, name="minus_sum")
             r["add"] = stat.tile([P, 1], F32, name="add")
             rows_of[i] = r
 
@@ -293,28 +287,34 @@ def tile_jointinputoutputembeddingtiedhead_d1p_kernel(
 
         def total(i):
             r = rows_of[i]
-            nc.vector.tensor_reduce(out=r["total"][:], in_=r["sums"][:, 0:3], axis=AX.X, op=ALU.add)
+            nc.vector.tensor_reduce(out=r["minus_sum"][:], in_=r["sums"][:, 0:3], axis=AX.X, op=ALU.add, negate=True)
 
-        def guess(i):
+        def newton(i, step):
             r = rows_of[i]
-            nc.vector.tensor_scalar(
-                out=r["y"][0][:],
-                in0=r["total"][:].bitcast(I32),
-                scalar1=LN2 / 2.0**23,
-                scalar2=-(127.0 - 0.043) * LN2 - SHIFT,
-                op0=ALU.mult,
-                op1=ALU.add,
-            )
-
-        def newton_exp(i, k):
-            r = rows_of[i]
-            nc.scalar.activation(out=r["e"][k][:], in_=r["y"][k][:], func=ACT.Exp, scale=-1.0, bias=k - SHIFT)
-
-        def newton_add(i, k):
-            r = rows_of[i]
-            nc.vector.scalar_tensor_tensor(
-                out=r["y"][k + 1][:], in0=r["e"][k][:], scalar=r["total"][:], in1=r["y"][k][:], op0=ALU.mult, op1=ALU.add
-            )
+            if step == 0:
+                bits = r["minus_sum"][:].bitcast(U32)
+                nc.scalar.activation(out=r["v0"][:], in_=bits, func=ACT.Identity, scale=-LN2 / 2.0**23, bias=GUESS)
+                nc.scalar.activation(
+                    out=r["e0"][:], in_=bits, func=ACT.Exp, scale=-LN2 / 2.0**23, bias=GUESS - 3.0 - math.log(V)
+                )
+            elif step in (1, 3):
+                k = step // 2
+                nc.scalar.activation(
+                    out=r["v%d" % (k + 1)][:],
+                    in_=r["e%d" % k][:],
+                    func=ACT.Identity,
+                    scale=r["minus_sum"][:],
+                    bias=r["v%d" % k][:],
+                )
+            elif step == 2:
+                nc.scalar.activation(out=r["e1"][:], in_=r["v1"][:], func=ACT.Exp, bias=1.0 - 3.0 - math.log(V))
+            elif step == 4:
+                nc.scalar.activation(out=r["e2"][:], in_=r["v2"][:], func=ACT.Exp, bias=2.0 - 3.0 - math.log(V))
+                nc.scalar.activation(out=r["near"][:], in_=r["v2"][:], func=ACT.Identity, bias=r["neg_top"][:])
+            else:
+                nc.scalar.activation(
+                    out=r["add"][:], in_=r["e2"][:], func=ACT.Identity, scale=r["minus_sum"][:], bias=r["near"][:]
+                )
 
         def vectors():
             nc.scalar.copy(
@@ -330,9 +330,6 @@ def tile_jointinputoutputembeddingtiedhead_d1p_kernel(
 
         def finish(i):
             r = rows_of[i]
-            nc.scalar.activation(
-                out=r["add"][:], in_=r["y"][3][:], func=ACT.Identity, scale=-1.0, bias=r["neg_top"][:]
-            )
             res = soft.tile([P, V], F32, name="res", bufs=5)
             if i < SHARED_FROM:
                 nc.gpsimd.tensor_scalar(
@@ -340,31 +337,25 @@ def tile_jointinputoutputembeddingtiedhead_d1p_kernel(
                 )
                 nc.sync.dma_start(out=out_view[i], in_=res[:])
             else:
-                a, b = 832, 1232
-                nc.vector.tensor_scalar(
-                    out=res[:, 0:a], in0=r["s"][:, 0:a], scalar1=r["add"][:], scalar2=None, op0=ALU.add
-                )
-                nc.sync.dma_start(out=out_view[i][:, 0:a], in_=res[:, 0:a])
-                nc.scalar.activation(
-                    out=res[:, a:b], in_=r["s"][:, a:b], func=ACT.Identity, bias=r["add"][:]
-                )
-                nc.sync.dma_start(out=out_view[i][:, a:b], in_=res[:, a:b])
-                nc.gpsimd.tensor_scalar(
-                    out=res[:, b:V], in0=r["s"][:, b:V], scalar1=1.0, scalar2=r["add"][:], op0=ALU.mult, op1=ALU.add
-                )
-                nc.sync.dma_start(out=out_view[i][:, b:V], in_=res[:, b:V])
+                for a in range(0, V, V // 2):
+                    cols = slice(a, a + V // 2)
+                    nc.vector.tensor_scalar(
+                        out=res[:, cols], in0=r["s"][:, cols], scalar1=r["add"][:], scalar2=None, op0=ALU.add
+                    )
+                    nc.sync.dma_start(out=out_view[i][:, cols], in_=res[:, cols])
 
         with tc.manual_schedule():
             turned = {}
-            for i in range(2 + 1):
-                if i < 2:
+            for i in range(4 + 1):
+                if i < 4:
                     turned[i] = turn(widen(i))
-                if i == 1:
+                if i == 2:
                     vectors()
+                if i == 2:
+                    permute_scales(u_sc_raw, u_sc)
+                    permute_words(u_raw, u_perm, 0)
                 if i >= 1:
                     gather(i - 1, turned[i - 1], i - 1 in GATHER_VECTOR)
-            permute_scales(u_sc_raw, u_sc)
-            permute_words(u_raw, u_perm, 0)
             groups = [(0, jg, cc) for cc in range(3) for jg in range(G)]
             groups += [(1, jg, cc) for cc in range(2) for jg in range(G)]
             planes_of = {}
@@ -374,17 +365,17 @@ def tile_jointinputoutputembeddingtiedhead_d1p_kernel(
             for n in range(len(groups) + 1):
                 if n < len(groups):
                     planes_of[n] = project(*groups[n])
-                for i in range(2, TILES):
+                for i in range(4, TILES):
                     if WIDEN_AT[i] == n:
                         rows_left[i] = widen(i)
                     if WIDEN_AT[i] + 1 == n:
                         turned[i] = turn(rows_left[i])
                     if WIDEN_AT[i] + 2 == n:
                         gather(i, turned[i], i in GATHER_VECTOR)
-                if n == 3:
+                if n == 1:
                     quantize_h(0, 0)
                     quantize_h(0, 1)
-                if n == 7:
+                if n == 6:
                     quantize_h(1, 0)
                     quantize_h(1, 1)
                 if n == 4:
@@ -394,50 +385,37 @@ def tile_jointinputoutputembeddingtiedhead_d1p_kernel(
                 if n == 0:
                     permute_words(u_raw, u_perm, 1)
                 if 1 <= n <= len(groups):
-                    rounded_of[n - 1] = apply_gain(n - 1, groups[n - 1][0], groups[n - 1][1], planes_of[n - 1])
-                if 3 <= n and n - 3 < 8:
-                    quantize_joint(*groups[n - 3], four_of[n - 3])
-                if 2 <= n and n - 2 < 8:
-                    four_of[n - 2] = interleave(rounded_of[n - 2])
+                    rounded_of[n - 1] = planes_of[n - 1]
+                    if GAIN_ENGINE[n - 1] == "A":
+                        rounded_of[n - 1] = scalar_gain(groups[n - 1][0], groups[n - 1][1], planes_of[n - 1])
+                m = n - 2
+                if 0 <= m < 8:
+                    quantize_joint(*groups[m], four_of[m])
+                m = n - 1
+                if 0 <= m < 8:
+                    four_of[m] = interleave(m, groups[m][0], groups[m][1], rounded_of[m])
             for r in range(TILES + 4):
-                new, old1, old2, old3, old4 = (x if 0 <= x < TILES else None for x in range(r, r - 5, -1))
-                if new is not None:
-                    start_tile(new)
+                new, old1, old2, old3 = (x if 0 <= x < TILES else None for x in range(r, r - 4, -1))
                 late = LATE.get(r)
                 if late is not None:
                     quantize_joint(*groups[late], four_of[late])
-                if old4 is not None:
-                    finish(old4)
-                if old3 is not None:
-                    newton_exp(old3, 1)
+                if new is not None:
+                    start_tile(new)
                 if old2 is not None:
                     total(old2)
-                if new is not None:
-                    take(new, 0, scores(new, 0))
-                if old1 is not None:
-                    exp_piece(old1, 0)
-                if old2 is not None:
-                    guess(old2)
+                for c in range(3):
+                    if new is not None:
+                        take(new, c, scores(new, c))
+                    if old1 is not None:
+                        exp_piece(old1, c)
+                    if old2 is not None:
+                        newton(old2, c)
+                    if old3 is not None:
+                        newton(old3, 3 + c)
+                    late = LATE.get(r + 1)
+                    if c == 0 and late is not None:
+                        four_of[late] = interleave(late, groups[late][0], groups[late][1], rounded_of[late])
                 if old3 is not None:
-                    newton_add(old3, 1)
-                late = LATE.get(r + 1)
-                if late is not None:
-                    four_of[late] = interleave(rounded_of[late])
-                if new is not None:
-                    take(new, 1, scores(new, 1))
-                if old1 is not None:
-                    exp_piece(old1, 1)
-                if old2 is not None:
-                    newton_exp(old2, 0)
-                if old3 is not None:
-                    newton_exp(old3, 2)
-                if new is not None:
-                    take(new, 2, scores(new, 2))
-                if old1 is not None:
-                    exp_piece(old1, 2)
-                if old2 is not None:
-                    newton_add(old2, 0)
-                if old3 is not None:
-                    newton_add(old3, 2)
+                    finish(old3)
                 if new is not None:
                     top(new)

@@ -23,12 +23,12 @@ G = 2
 COLS = 512
 TILES = N // P
 KB = D // 128
-WIDEN_VECTOR = (8, 8, 6, 6, 4, 4, 4, 4)
-GATHER_VECTOR = (98, 99)
-SHARED_FROM = 5
+WIDEN_VECTOR = (8, 7, 2, 8, 2, 5, 8, 6)
+GATHER_VECTOR = (4, 0, 1, 98, 99)
+SHARED_FROM = 4
 GAIN_ENGINE = "VVVVVVVVAA"
 LATE = {1: 8, 3: 9}
-WIDEN_AT = {4: 0, 5: 1, 6: 2, 7: 3}
+WIDEN_AT = {4: 0, 5: 1, 6: 3, 7: 1}
 LN2 = math.log(2.0)
 GUESS = (256.0 + 127.0 - 0.043) * LN2 + math.log(V) + 3.0
 
@@ -98,8 +98,8 @@ def tile_jointinputoutputembeddingtiedhead_d1p_kernel(
         load_h(2)
         load_h(3)
         load_words(emb_words, 1, e_words[1])
-        load_words(emb_words, 2, e_words[2])
         load_words(vp_words, 0, v_raw[0])
+        load_words(emb_words, 2, e_words[2])
         load_words(vp_words, 1, v_raw[1])
         load_scales(nc.gpsimd, v_sc_raw, vp_scales)
         nc.scalar.activation(out=warm_out[:], in_=warm[:], func=ACT.Tanh)
@@ -174,7 +174,7 @@ def tile_jointinputoutputembeddingtiedhead_d1p_kernel(
         ctx_scales = keep.tile([P, G, N], U8, align_bytes=64)
 
         def project(side, jg, cc):
-            planes = work.tile([P, 4, COLS], F32, name="planes", bufs=3)
+            planes = work.tile([P, 4, COLS], F32, name="planes", bufs=4)
             w, wsc = (u_perm, u_sc) if side == 0 else (v_perm, v_sc)
             for t in range(4):
                 bank = banks.tile([P, COLS], F32, name="bank")
@@ -200,19 +200,23 @@ def tile_jointinputoutputembeddingtiedhead_d1p_kernel(
                 )
             return planes
 
-        def scalar_gain(side, jg, planes):
+        def early_gain(n, side, jg, planes):
             rounded = work.tile([P, 4, COLS], BF16, align_bytes=64, name="rounded", bufs=2)
             for t in range(4):
-                nc.scalar.activation(
-                    out=rounded[:, t, :], in_=planes[:, t, :], func=ACT.Copy, scale=vecs[:, 4 + 2 * side + jg, t : t + 1]
-                )
+                dst, src, gain = rounded[:, t, :], planes[:, t, :], vecs[:, 4 + 2 * side + jg, t : t + 1]
+                if GAIN_ENGINE[n] in "AB":
+                    nc.scalar.activation(out=dst, in_=src, func=ACT.Copy, scale=gain)
+                else:
+                    nc.gpsimd.tensor_scalar(out=dst, in0=src, scalar1=gain, scalar2=0.0, op0=ALU.mult, op1=ALU.add)
             return rounded
 
         def interleave(n, side, jg, source):
             four = work.tile([P, COLS, 4], BF16, align_bytes=64, name="four", bufs=3)
             dst = four[:].rearrange("p (c i) t -> p c t i", i=4)
             src = source[:].rearrange("p t (c i) -> p c t i", i=4)
-            if GAIN_ENGINE[n] == "A":
+            if GAIN_ENGINE[n] == "B":
+                nc.scalar.copy(out=dst, in_=src)
+            elif GAIN_ENGINE[n] != "V":
                 nc.vector.tensor_copy(out=dst, in_=src)
             else:
                 gain = vecs[:, 4 + 2 * side + jg, :].unsqueeze(1).unsqueeze(3).to_broadcast([P, COLS // 4, 4, 4])
@@ -289,7 +293,7 @@ def tile_jointinputoutputembeddingtiedhead_d1p_kernel(
             r = rows_of[i]
             nc.vector.tensor_reduce(out=r["minus_sum"][:], in_=r["sums"][:, 0:3], axis=AX.X, op=ALU.add, negate=True)
 
-        def newton(i, step):
+        def logarithm(i, step):
             r = rows_of[i]
             if step == 0:
                 bits = r["minus_sum"][:].bitcast(U32)
@@ -330,15 +334,15 @@ def tile_jointinputoutputembeddingtiedhead_d1p_kernel(
 
         def finish(i):
             r = rows_of[i]
-            res = soft.tile([P, V], F32, name="res", bufs=5)
+            res = soft.tile([P, V], F32, name="res", bufs=4)
             if i < SHARED_FROM:
                 nc.gpsimd.tensor_scalar(
                     out=res[:], in0=r["s"][:], scalar1=1.0, scalar2=r["add"][:], op0=ALU.mult, op1=ALU.add
                 )
                 nc.sync.dma_start(out=out_view[i], in_=res[:])
             else:
-                for a in range(0, V, V // 2):
-                    cols = slice(a, a + V // 2)
+                for a in range(0, V, V // 3):
+                    cols = slice(a, a + V // 3)
                     nc.vector.tensor_scalar(
                         out=res[:, cols], in0=r["s"][:, cols], scalar1=r["add"][:], scalar2=None, op0=ALU.add
                     )
@@ -351,7 +355,7 @@ def tile_jointinputoutputembeddingtiedhead_d1p_kernel(
                     turned[i] = turn(widen(i))
                 if i == 2:
                     vectors()
-                if i == 2:
+                if i == 4:
                     permute_scales(u_sc_raw, u_sc)
                     permute_words(u_raw, u_perm, 0)
                 if i >= 1:
@@ -378,7 +382,7 @@ def tile_jointinputoutputembeddingtiedhead_d1p_kernel(
                 if n == 6:
                     quantize_h(1, 0)
                     quantize_h(1, 1)
-                if n == 4:
+                if n == 2:
                     permute_scales(v_sc_raw, v_sc)
                     permute_words(v_raw, v_perm, 0)
                     permute_words(v_raw, v_perm, 1)
@@ -386,14 +390,14 @@ def tile_jointinputoutputembeddingtiedhead_d1p_kernel(
                     permute_words(u_raw, u_perm, 1)
                 if 1 <= n <= len(groups):
                     rounded_of[n - 1] = planes_of[n - 1]
-                    if GAIN_ENGINE[n - 1] == "A":
-                        rounded_of[n - 1] = scalar_gain(groups[n - 1][0], groups[n - 1][1], planes_of[n - 1])
-                m = n - 2
-                if 0 <= m < 8:
-                    quantize_joint(*groups[m], four_of[m])
+                    if GAIN_ENGINE[n - 1] != "V":
+                        rounded_of[n - 1] = early_gain(n - 1, groups[n - 1][0], groups[n - 1][1], planes_of[n - 1])
                 m = n - 1
                 if 0 <= m < 8:
                     four_of[m] = interleave(m, groups[m][0], groups[m][1], rounded_of[m])
+                m = n - 2
+                if 0 <= m < 8:
+                    quantize_joint(*groups[m], four_of[m])
             for r in range(TILES + 4):
                 new, old1, old2, old3 = (x if 0 <= x < TILES else None for x in range(r, r - 4, -1))
                 late = LATE.get(r)
@@ -403,19 +407,21 @@ def tile_jointinputoutputembeddingtiedhead_d1p_kernel(
                     start_tile(new)
                 if old2 is not None:
                     total(old2)
+                if old3 is not None:
+                    logarithm(old3, 3)
                 for c in range(3):
                     if new is not None:
                         take(new, c, scores(new, c))
                     if old1 is not None:
                         exp_piece(old1, c)
                     if old2 is not None:
-                        newton(old2, c)
-                    if old3 is not None:
-                        newton(old3, 3 + c)
+                        logarithm(old2, c)
+                    if old3 is not None and c < 2:
+                        logarithm(old3, 4 + c)
                     late = LATE.get(r + 1)
                     if c == 0 and late is not None:
                         four_of[late] = interleave(late, groups[late][0], groups[late][1], rounded_of[late])
-                if old3 is not None:
-                    finish(old3)
+                    if old3 is not None and c == 2:
+                        finish(old3)
                 if new is not None:
                     top(new)

@@ -23,12 +23,12 @@ G = 2
 COLS = 512
 TILES = N // P
 KB = D // 128
-WIDEN_VECTOR = (8, 7, 2, 8, 2, 5, 8, 6)
+WIDEN_VECTOR = (8, 8, 3, 8, 5, 4, 6, 4)
 GATHER_VECTOR = (4, 0, 1, 98, 99)
 SHARED_FROM = 4
 GAIN_ENGINE = "VVVVVVVVAA"
 LATE = {1: 8, 3: 9}
-WIDEN_AT = {4: 0, 5: 1, 6: 3, 7: 1}
+WIDEN_AT = {4: 0, 5: 1, 6: 2, 7: 1}
 LN2 = math.log(2.0)
 GUESS = (256.0 + 127.0 - 0.043) * LN2 + math.log(V) + 3.0
 
@@ -355,7 +355,7 @@ def tile_jointinputoutputembeddingtiedhead_d1p_kernel(
                     turned[i] = turn(widen(i))
                 if i == 2:
                     vectors()
-                if i == 4:
+                if i == 3:
                     permute_scales(u_sc_raw, u_sc)
                     permute_words(u_raw, u_perm, 0)
                 if i >= 1:
@@ -379,7 +379,7 @@ def tile_jointinputoutputembeddingtiedhead_d1p_kernel(
                 if n == 1:
                     quantize_h(0, 0)
                     quantize_h(0, 1)
-                if n == 6:
+                if n == 7:
                     quantize_h(1, 0)
                     quantize_h(1, 1)
                 if n == 2:
@@ -403,17 +403,18 @@ def tile_jointinputoutputembeddingtiedhead_d1p_kernel(
                 late = LATE.get(r)
                 if late is not None:
                     quantize_joint(*groups[late], four_of[late])
-                if new is not None:
-                    start_tile(new)
-                if old2 is not None:
-                    total(old2)
-                if old3 is not None:
-                    logarithm(old3, 3)
+                if r == 0:
+                    start_tile(0)
+                    take(0, 0, scores(0, 0))
                 for c in range(3):
-                    if new is not None:
-                        take(new, c, scores(new, c))
+                    if new is not None and c < 2:
+                        take(new, c + 1, scores(new, c + 1))
+                    if c == 0 and old2 is not None:
+                        total(old2)
                     if old1 is not None:
                         exp_piece(old1, c)
+                    if c == 0 and old3 is not None:
+                        logarithm(old3, 3)
                     if old2 is not None:
                         logarithm(old2, c)
                     if old3 is not None and c < 2:
@@ -423,5 +424,8 @@ def tile_jointinputoutputembeddingtiedhead_d1p_kernel(
                         four_of[late] = interleave(late, groups[late][0], groups[late][1], rounded_of[late])
                     if old3 is not None and c == 2:
                         finish(old3)
-                if new is not None:
-                    top(new)
+                    if c == 1 and r + 1 < TILES:
+                        start_tile(r + 1)
+                        take(r + 1, 0, scores(r + 1, 0))
+                    if c == 1 and new is not None:
+                        top(new)

import math
from contextlib import ExitStack

import concourse.mybir as mybir
from concourse.masks import make_identity

N, D, J, V = 1024, 1024, 1024, 1536
FLOPS = 2 * (V * D * J + N * D * J + N * J * V)

F32 = mybir.dt.float32
BF16 = mybir.dt.bfloat16
I32 = mybir.dt.int32
U32 = mybir.dt.uint32
U8 = mybir.dt.uint8
FP8 = mybir.dt.float8_e4m3fn
X4 = mybir.dt.float8_e4m3fn_x4
ACT = mybir.ActivationFunctionType
ALU = mybir.AluOpType
AX = mybir.AxisListType

P = 128
G = 2
COLS = 512
TILES = N // P
KB = D // 128
WIDEN_VECTOR = (8, 8, 3, 8, 5, 4, 6, 4)
GATHER_VECTOR = (4, 0, 1, 98, 99)
SHARED_FROM = 4
GAIN_ENGINE = "VVVVVVVVAA"
LATE = {1: 8, 3: 9}
WIDEN_AT = {4: 0, 5: 1, 6: 2, 7: 1}
LN2 = math.log(2.0)
GUESS = (256.0 + 127.0 - 0.043) * LN2 + math.log(V) + 3.0


def tile_jointinputoutputembeddingtiedhead_d1p_kernel(
    tc, h_bytes, h_scale, emb_words, emb_scales, u_words, u_scales, vp_words, vp_scales, bj, gu, gv, out
):
    nc = tc.nc
    with ExitStack() as ctx:
        keep = ctx.enter_context(tc.tile_pool(name="keep", bufs=1))
        work = ctx.enter_context(tc.tile_pool(name="work", bufs=3))
        stat = ctx.enter_context(tc.tile_pool(name="stat", bufs=6))
        soft = ctx.enter_context(tc.tile_pool(name="soft", bufs=4))
        banks = ctx.enter_context(tc.psum_pool(name="banks", bufs=8))

        warm_out = keep.tile([P, 1], F32)

        u_sc_raw = keep.tile([P, J], U8, align_bytes=64)
        v_sc_raw = keep.tile([P, J], U8, align_bytes=64)
        e_sc = keep.tile([P, V], U8, align_bytes=64)
        nc.vector.memset(u_sc_raw[:].bitcast(I32), 0)
        vec_raw = keep.tile([P, 512], BF16)
        nc.vector.memset(vec_raw[:].bitcast(I32), 0)
        nc.vector.memset(e_sc[:].bitcast(I32), 0)
        nc.vector.memset(v_sc_raw[:].bitcast(I32), 0)
        warm = keep.tile([P, 1], F32)
        nc.vector.memset(warm[:], 0.0)
        def load_scales(queue, tile_, src, quadrants=range(4)):
            for q in quadrants:
                queue.dma_start(
                    out=tile_[32 * q : 32 * q + 8, :].bitcast(I32),
                    in_=src[:, 4 * q : 4 * q + 4, :].bitcast(I32),
                )

        ident = keep.tile([P, P], F32)
        make_identity(nc, ident[:])
        hs = keep.tile([P, TILES * KB], F32)
        h_view = h_bytes.rearrange("(p i) k -> p (i k)", i=TILES)
        nc.sync.dma_start(out=hs[:], in_=h_scale.rearrange("(p i) b -> p (i b)", i=TILES))
        h_raw = []
        for pair in range(4):
            h_two = keep.tile([P, 2 * D], U8, align_bytes=64, name="h_raw%d" % pair)
            h_raw.append(h_two)

        def load_h(pair):
            nc.sync.dma_start(out=h_raw[pair][:], in_=h_view[:, 2 * D * pair : 2 * D * (pair + 1)])

        u_raw = [keep.tile([P, G, COLS], I32, align_bytes=64, name="u_raw%d" % b) for b in range(2)]
        v_raw = [keep.tile([P, G, COLS], I32, align_bytes=64, name="v_raw%d" % b) for b in range(2)]
        e_words = [keep.tile([P, G, COLS], I32, align_bytes=64, name="e_words%d" % c) for c in range(3)]

        def load_words(src, block, tile_):
            words = src.rearrange("g p n t -> p g (n t)").bitcast(I32)
            nc.sync.dma_start(out=tile_[:], in_=words[:, :, COLS * block : COLS * (block + 1)])

        load_h(0)
        load_h(1)
        load_words(u_words, 0, u_raw[0])
        nc.scalar.dma_start(out=vec_raw[0:4, :], in_=bj.rearrange("s j -> (s j)").rearrange("(x m) -> x m", x=4))
        nc.scalar.dma_start(out=vec_raw[4:6, :], in_=gu.rearrange("(x m) -> x m", x=2))
        nc.scalar.dma_start(out=vec_raw[6:8, :], in_=gv.rearrange("(x m) -> x m", x=2))
        load_scales(nc.scalar, u_sc_raw, u_scales)
        load_scales(nc.scalar, e_sc, emb_scales, range(2, 4))
        load_scales(nc.gpsimd, e_sc, emb_scales, range(2))
        load_words(emb_words, 0, e_words[0])
        load_words(u_words, 1, u_raw[1])
        load_h(2)
        load_h(3)
        load_words(emb_words, 1, e_words[1])
        load_words(vp_words, 0, v_raw[0])
        load_words(emb_words, 2, e_words[2])
        load_words(vp_words, 1, v_raw[1])
        load_scales(nc.gpsimd, v_sc_raw, vp_scales)
        nc.scalar.activation(out=warm_out[:], in_=warm[:], func=ACT.Tanh)

        vec_rows = keep.tile([P, 512], F32)
        vecs = keep.tile([P, 8, 4], F32)
        u_perm = [keep.tile([P, G, COLS], I32, align_bytes=64, name="u_perm%d" % b) for b in range(2)]
        v_perm = [keep.tile([P, G, COLS], I32, align_bytes=64, name="v_perm%d" % b) for b in range(2)]
        u_sc = keep.tile([P, J], U8, align_bytes=64)
        v_sc = keep.tile([P, J], U8, align_bytes=64)

        def permute_words(raw, dst, b):
            nc.vector.tensor_copy(
                out=dst[b][:].rearrange("p g (t q i) -> p g t q i", t=4, i=8),
                in_=raw[b][:].rearrange("p g (q t i) -> p g t q i", t=4, i=8),
            )

        def permute_scales(sc_raw, sc_dst):
            nc.vector.tensor_copy(
                out=sc_dst[:].bitcast(I32).rearrange("p (b t q i) -> p b t q i", b=2, t=4, i=2),
                in_=sc_raw[:].bitcast(I32).rearrange("p (b q t i) -> p b t q i", b=2, t=4, i=2),
            )

        h_grp = []
        for half in range(2):
            h_four = keep.tile([P, G, COLS, 2], F32, align_bytes=64, name="h_grp%d" % half)
            h_grp.append(h_four)
        h_codes = keep.tile([P, G, N], U32, align_bytes=64)
        h_scales = keep.tile([P, G, N], U8, align_bytes=64)

        def widen(i):
            rows = work.tile([P, D], BF16, name="rows")
            for j in range(KB):
                at = D * (i % 2) + 128 * j
                src = h_raw[i // 2][:, at : at + 128].bitcast(FP8)
                dst = rows[:, 128 * j : 128 * (j + 1)]
                col = hs[:, KB * i + j : KB * i + j + 1]
                if j < WIDEN_VECTOR[i]:
                    nc.vector.tensor_scalar(out=dst, in0=src, scalar1=col, scalar2=None, op0=ALU.mult)
                else:
                    nc.scalar.activation(out=dst, in_=src, func=ACT.Copy, scale=col)
            return rows

        def turn(rows):
            words = rows[:].bitcast(F32)
            bank = banks.tile([P, COLS], F32, name="bank")
            for g in range(G):
                for e in range(2):
                    s0 = 128 * (2 * g + e)
                    nc.tensor.transpose(bank[:, s0 : s0 + 128], words[:, 256 * g + e : 256 * (g + 1) : 2], ident[:])
            return bank

        def gather(i, bank, vector):
            dst = h_grp[i // 4][:, :, 128 * (i % 4) : 128 * (i % 4 + 1), :]
            src = bank[:].rearrange("p (g e r) -> p g r e", g=2, e=2)
            if vector:
                nc.vector.tensor_copy(out=dst, in_=src)
            else:
                nc.scalar.copy(out=dst, in_=src)

        def quantize_h(half, g):
            cols = slice(COLS * half, COLS * (half + 1))
            nc.vector.quantize_mx(
                out=h_codes[:, g, cols].bitcast(X4),
                scales=h_scales[:, g, cols],
                in_=h_grp[half][:, g].rearrange("p r e -> p (r e)").bitcast(BF16),
            )

        lab_codes = keep.tile([P, G, V], U32, align_bytes=64)
        lab_scales = keep.tile([P, G, V], U8, align_bytes=64)
        ctx_codes = keep.tile([P, G, N], U32, align_bytes=64)
        ctx_scales = keep.tile([P, G, N], U8, align_bytes=64)

        def project(side, jg, cc):
            planes = work.tile([P, 4, COLS], F32, name="planes", bufs=4)
            w, wsc = (u_perm, u_sc) if side == 0 else (v_perm, v_sc)
            for t in range(4):
                bank = banks.tile([P, COLS], F32, name="bank")
                wcols = slice(512 * jg + 128 * t, 512 * jg + 128 * (t + 1))
                for g in range(G):
                    if side == 0:
                        rhs = e_words[cc][:, g, :].bitcast(X4)
                        rhs_scale = e_sc[4 * g :, COLS * cc : COLS * (cc + 1)]
                    else:
                        rhs = h_codes[:, g, COLS * cc : COLS * (cc + 1)].bitcast(X4)
                        rhs_scale = h_scales[:, g, COLS * cc : COLS * (cc + 1)]
                    nc.tensor.matmul_mx(
                        out=bank[:],
                        lhsT=w[jg][:, g, 128 * t : 128 * (t + 1)].bitcast(X4),
                        lhsT_scale=wsc[4 * g :, wcols],
                        rhs=rhs,
                        rhs_scale=rhs_scale,
                        start=(g == 0),
                        stop=(g == G - 1),
                    )
                nc.scalar.activation(
                    out=planes[:, t, :], in_=bank[:], func=ACT.Tanh, bias=vecs[:, 2 * side + jg, t : t + 1]
                )
            return planes

        def early_gain(n, side, jg, planes):
            rounded = work.tile([P, 4, COLS], BF16, align_bytes=64, name="rounded", bufs=2)
            for t in range(4):
                dst, src, gain = rounded[:, t, :], planes[:, t, :], vecs[:, 4 + 2 * side + jg, t : t + 1]
                if GAIN_ENGINE[n] in "AB":
                    nc.scalar.activation(out=dst, in_=src, func=ACT.Copy, scale=gain)
                else:
                    nc.gpsimd.tensor_scalar(out=dst, in0=src, scalar1=gain, scalar2=0.0, op0=ALU.mult, op1=ALU.add)
            return rounded

        def interleave(n, side, jg, source):
            four = work.tile([P, COLS, 4], BF16, align_bytes=64, name="four", bufs=3)
            dst = four[:].rearrange("p (c i) t -> p c t i", i=4)
            src = source[:].rearrange("p t (c i) -> p c t i", i=4)
            if GAIN_ENGINE[n] == "B":
                nc.scalar.copy(out=dst, in_=src)
            elif GAIN_ENGINE[n] != "V":
                nc.vector.tensor_copy(out=dst, in_=src)
            else:
                gain = vecs[:, 4 + 2 * side + jg, :].unsqueeze(1).unsqueeze(3).to_broadcast([P, COLS // 4, 4, 4])
                nc.vector.tensor_tensor(out=dst, in0=src, in1=gain, op=ALU.mult)
            return four

        def quantize_joint(side, jg, cc, four):
            codes, scales = (lab_codes, lab_scales) if side == 0 else (ctx_codes, ctx_scales)
            cols = slice(COLS * cc, COLS * (cc + 1))
            nc.vector.quantize_mx(
                out=codes[:, jg, cols].bitcast(X4),
                scales=scales[:, jg, cols],
                in_=four[:].rearrange("p c t -> p (c t)"),
            )

        out_view = out.rearrange("(p i) v -> i p v", i=TILES)

        def scores(i, c):
            bank = banks.tile([P, COLS], F32, name="bank")
            for g in range(G):
                nc.tensor.matmul_mx(
                    out=bank[:],
                    lhsT=ctx_codes[:, g, P * i : P * (i + 1)].bitcast(X4),
                    lhsT_scale=ctx_scales[:, g, P * i : P * (i + 1)],
                    rhs=lab_codes[:, g, COLS * c : COLS * (c + 1)].bitcast(X4),
                    rhs_scale=lab_scales[:, g, COLS * c : COLS * (c + 1)],
                    start=(g == 0),
                    stop=(g == G - 1),
                )
            return bank

        rows_of = {}

        def start_tile(i):
            r = {}
            r["s"] = soft.tile([P, V], F32, name="s", bufs=6)
            r["tops"] = stat.tile([P, 8], F32, name="tops")
            r["sums"] = stat.tile([P, 8], F32, name="sums")
            for key in ("v0", "v1", "v2", "e0", "e1", "e2", "near"):
                r[key] = stat.tile([P, 1], F32, name=key)
            r["neg_top"] = stat.tile([P, 1], F32, name="neg_top")
            r["minus_sum"] = stat.tile([P, 1], F32, name="minus_sum")
            r["add"] = stat.tile([P, 1], F32, name="add")
            rows_of[i] = r

        def take(i, c, bank):
            r = rows_of[i]
            nc.vector.tensor_scalar(
                out=r["s"][:, COLS * c : COLS * (c + 1)],
                in0=bank[:],
                scalar1=2.0 / math.sqrt(J),
                scalar2=None,
                op0=ALU.mult,
                op1=ALU.max,
                accum_out=r["tops"][:, c : c + 1],
            )

        def top(i):
            r = rows_of[i]
            nc.vector.tensor_reduce(out=r["neg_top"][:], in_=r["tops"][:, 0:3], axis=AX.X, op=ALU.max, negate=True)

        def exp_piece(i, c):
            r = rows_of[i]
            junk = work.tile([P, COLS], BF16, name="junk")
            nc.scalar.activation(
                out=junk[:],
                in_=r["s"][:, COLS * c : COLS * (c + 1)],
                func=ACT.Exp,
                bias=r["neg_top"][:],
                accum_out=r["sums"][:, c : c + 1],
            )

        def total(i):
            r = rows_of[i]
            nc.vector.tensor_reduce(out=r["minus_sum"][:], in_=r["sums"][:, 0:3], axis=AX.X, op=ALU.add, negate=True)

        def logarithm(i, step):
            r = rows_of[i]
            if step == 0:
                bits = r["minus_sum"][:].bitcast(U32)
                nc.scalar.activation(out=r["v0"][:], in_=bits, func=ACT.Identity, scale=-LN2 / 2.0**23, bias=GUESS)
                nc.scalar.activation(
                    out=r["e0"][:], in_=bits, func=ACT.Exp, scale=-LN2 / 2.0**23, bias=GUESS - 3.0 - math.log(V)
                )
            elif step in (1, 3):
                k = step // 2
                nc.scalar.activation(
                    out=r["v%d" % (k + 1)][:],
                    in_=r["e%d" % k][:],
                    func=ACT.Identity,
                    scale=r["minus_sum"][:],
                    bias=r["v%d" % k][:],
                )
            elif step == 2:
                nc.scalar.activation(out=r["e1"][:], in_=r["v1"][:], func=ACT.Exp, bias=1.0 - 3.0 - math.log(V))
            elif step == 4:
                nc.scalar.activation(out=r["e2"][:], in_=r["v2"][:], func=ACT.Exp, bias=2.0 - 3.0 - math.log(V))
                nc.scalar.activation(out=r["near"][:], in_=r["v2"][:], func=ACT.Identity, bias=r["neg_top"][:])
            else:
                nc.scalar.activation(
                    out=r["add"][:], in_=r["e2"][:], func=ACT.Identity, scale=r["minus_sum"][:], bias=r["near"][:]
                )

        def vectors():
            nc.scalar.copy(
                out=vec_rows[:].rearrange("p (t q i) -> p t q i", t=4, i=8),
                in_=vec_raw[:].rearrange("p (q t i) -> p t q i", t=4, i=8),
            )
            bank = banks.tile([P, COLS], F32, name="bank")
            for t in range(4):
                nc.tensor.transpose(bank[:, 128 * t : 128 * (t + 1)], vec_rows[:, 128 * t : 128 * (t + 1)], ident[:])
            nc.scalar.copy(
                out=vecs[:], in_=bank[:].rearrange("p (t r) -> p r t", t=4)[:, 0:8, :]
            )

        def finish(i):
            r = rows_of[i]
            res = soft.tile([P, V], F32, name="res", bufs=4)
            if i < SHARED_FROM:
                nc.gpsimd.tensor_scalar(
                    out=res[:], in0=r["s"][:], scalar1=1.0, scalar2=r["add"][:], op0=ALU.mult, op1=ALU.add
                )
                nc.sync.dma_start(out=out_view[i], in_=res[:])
            else:
                for a in range(0, V, V // 3):
                    cols = slice(a, a + V // 3)
                    nc.vector.tensor_scalar(
                        out=res[:, cols], in0=r["s"][:, cols], scalar1=r["add"][:], scalar2=None, op0=ALU.add
                    )
                    nc.sync.dma_start(out=out_view[i][:, cols], in_=res[:, cols])

        with tc.manual_schedule():
            turned = {}
            for i in range(4 + 1):
                if i < 4:
                    turned[i] = turn(widen(i))
                if i == 2:
                    vectors()
                if i == 3:
                    permute_scales(u_sc_raw, u_sc)
                    permute_words(u_raw, u_perm, 0)
                if i >= 1:
                    gather(i - 1, turned[i - 1], i - 1 in GATHER_VECTOR)
            groups = [(0, jg, cc) for cc in range(3) for jg in range(G)]
            groups += [(1, jg, cc) for cc in range(2) for jg in range(G)]
            planes_of = {}
            rounded_of = {}
            four_of = {}
            rows_left = {}
            for n in range(len(groups) + 1):
                if n < len(groups):
                    planes_of[n] = project(*groups[n])
                for i in range(4, TILES):
                    if WIDEN_AT[i] == n:
                        rows_left[i] = widen(i)
                    if WIDEN_AT[i] + 1 == n:
                        turned[i] = turn(rows_left[i])
                    if WIDEN_AT[i] + 2 == n:
                        gather(i, turned[i], i in GATHER_VECTOR)
                if n == 1:
                    quantize_h(0, 0)
                    quantize_h(0, 1)
                if n == 7:
                    quantize_h(1, 0)
                    quantize_h(1, 1)
                if n == 2:
                    permute_scales(v_sc_raw, v_sc)
                    permute_words(v_raw, v_perm, 0)
                    permute_words(v_raw, v_perm, 1)
                if n == 0:
                    permute_words(u_raw, u_perm, 1)
                if 1 <= n <= len(groups):
                    rounded_of[n - 1] = planes_of[n - 1]
                    if GAIN_ENGINE[n - 1] != "V":
                        rounded_of[n - 1] = early_gain(n - 1, groups[n - 1][0], groups[n - 1][1], planes_of[n - 1])
                m = n - 1
                if 0 <= m < 8:
                    four_of[m] = interleave(m, groups[m][0], groups[m][1], rounded_of[m])
                m = n - 2
                if 0 <= m < 8:
                    quantize_joint(*groups[m], four_of[m])
            for r in range(TILES + 4):
                new, old1, old2, old3 = (x if 0 <= x < TILES else None for x in range(r, r - 4, -1))
                late = LATE.get(r)
                if late is not None:
                    quantize_joint(*groups[late], four_of[late])
                if r == 0:
                    start_tile(0)
                    take(0, 0, scores(0, 0))
                for c in range(3):
                    if new is not None and c < 2:
                        take(new, c + 1, scores(new, c + 1))
                    if c == 0 and old2 is not None:
                        total(old2)
                    if old1 is not None:
                        exp_piece(old1, c)
                    if c == 0 and old3 is not None:
                        logarithm(old3, 3)
                    if old2 is not None:
                        logarithm(old2, c)
                    if old3 is not None and c < 2:
                        logarithm(old3, 4 + c)
                    late = LATE.get(r + 1)
                    if c == 0 and late is not None:
                        four_of[late] = interleave(late, groups[late][0], groups[late][1], rounded_of[late])
                    if old3 is not None and c == 2:
                        finish(old3)
                    if c == 1 and r + 1 < TILES:
                        start_tile(r + 1)
                        take(r + 1, 0, scores(r + 1, 0))
                    if c == 1 and new is not None:
                        top(new)
